import numpy as np
import ml_dtypes


def mxq(x, axis, fmt="e4m3"):
    dtype, down = {"e4m3": (ml_dtypes.float8_e4m3fn, 7), "e5m2": (ml_dtypes.float8_e5m2, 14)}[fmt]
    v = np.moveaxis(np.asarray(x, np.float32).astype(ml_dtypes.bfloat16).astype(np.float64), axis, -1)
    blocks = v.reshape(v.shape[:-1] + (-1, 32))
    amax = np.abs(blocks).max(-1, keepdims=True)
    byte = np.maximum(np.where(amax > 0, np.frexp(amax)[1] - 1 + 127, 0) - down, 1)
    scale = np.exp2(byte - 127.0)
    codes = (blocks / scale).astype(np.float32).astype(dtype).astype(np.float64)
    return np.moveaxis((codes * scale).reshape(v.shape), -1, axis)


WIDE = False


def mx_kscale(k):
    if not WIDE:
        return np.ones(k)
    levels = np.array([10, -10, 5, -5, 0])
    if k % 512:
        return np.exp2(np.random.permutation(np.resize(levels, k // 32))).repeat(32)
    a = np.empty((k // 512, 16))
    for p in range(k // 512):
        a[p, :8] = np.random.permutation(np.resize(levels, 8))
        for g in range(8):
            far = levels[np.abs(levels - a[p, g]) >= 10]
            a[p, g + 8] = far[np.random.randint(len(far))]
    return np.exp2(a.ravel()).repeat(32)


def f64(x):
    return np.asarray(x).astype(np.float64)


def striped(idx):
    return np.tile(np.asarray(idx).reshape(-1, 16).T, (8, 1)).astype(np.uint16)


def unstriped(offs):
    return offs[:16].T.reshape(-1).astype(np.int64)


def striped8(idx):
    return np.asarray(idx).reshape(8, -1, 16).transpose(0, 2, 1).reshape(128, -1).astype(np.uint16)


def unstriped8(offs):
    return offs.reshape(8, 16, -1).transpose(0, 2, 1).reshape(8, -1).astype(np.int64)


def pick8(x, idx, run):
    r = np.arange(len(x))
    return x[r[:, None], idx[r % (8 * run) // run]]


E2M1 = np.array([0.0, 0.5, 1.0, 1.5, 2.0, 3.0, 4.0, 6.0, -0.0, -0.5, -1.0, -1.5, -2.0, -3.0, -4.0, -6.0])


def pack_weight(w, fmt):
    k, n = w.shape
    w = f64(np.asarray(w, np.float32).astype(ml_dtypes.bfloat16)).reshape(k // 32, 32, n)
    amax = np.abs(w).max(1)
    if fmt == "e4m3":
        byte = np.frexp(amax)[1] - 1 + 127 - 7
    else:
        mant, ex = np.frexp(amax / 6.0)
        byte = np.where(mant > 0.5, ex, ex - 1) + 127
    byte = np.clip(np.where(amax > 0, byte, 1), 1, 254)
    scaled = (w * np.exp2(127.0 - byte)[:, None, :]).reshape(k, n).astype(np.float32)
    by_word = np.ascontiguousarray(scaled.reshape(k // 512, 128, 4, n).transpose(0, 1, 3, 2))
    if fmt == "e4m3":
        words = by_word.astype(ml_dtypes.float8_e4m3fn).view(np.uint8)
    else:
        c = by_word.astype(ml_dtypes.float4_e2m1fn).view(np.uint8) & 0xF
        words = (c[..., 0::2] | (c[..., 1::2] << 4)).reshape(k // 512, 128, 2 * n)
    return np.ascontiguousarray(words), np.ascontiguousarray(byte.astype(np.uint8).reshape(k // 512, 16, n))


def unpack_weight(words, scales, fmt):
    g, _, n = scales.shape
    words = np.ascontiguousarray(words).reshape(g, 128, n, -1)
    if fmt == "e4m3":
        vals = words.view(ml_dtypes.float8_e4m3fn).astype(np.float64)
    else:
        nib = np.empty((g, 128, n, 4), np.uint8)
        nib[..., 0::2] = words & 0xF
        nib[..., 1::2] = words >> 4
        vals = E2M1[nib]
    vals = vals * np.repeat(np.exp2(scales.astype(np.float64) - 127.0), 8, axis=1)[..., None]
    return vals.transpose(0, 1, 3, 2).reshape(g * 512, n)


K, J, R, T, U, F, O, S, N = 512, 512, 512, 2048, 1024, 1024, 128, 256, 256


def setup_inputs():
    n = np.random.standard_normal
    idx = np.stack([np.random.permutation(T)[:U] for _ in range(8)])
    idx2 = np.random.permutation(U)[:J]
    idx3 = np.stack([np.random.permutation(U)[:J] for _ in range(8)])
    idx4 = np.random.permutation(F)[:R]
    idx5 = np.stack([np.random.permutation(J)[:S] for _ in range(8)])
    idx6 = np.stack([np.random.permutation(S)[:O] for _ in range(8)])
    idx7 = np.random.permutation(S)[:O]
    fk = mx_kscale(K)
    fr = mx_kscale(R)
    tr = np.ones(F)
    tr[idx4] = fr
    wtp = pack_weight(n((K, F)) * 1 / np.sqrt(K) / fk[:, None] * tr, "e2m1")
    wbp = pack_weight(n((R, N)) * 1 / np.sqrt(R) / fr[:, None], "e4m3")
    return {
        "ta": (np.random.randint(-7, 8, (K, T)).astype(np.float64)).astype(np.float32),
        "ga": ((np.random.randint(8, 25, (K, 1)) / 64.0) * fk[:, None]).astype(np.float32),
        "gb": (np.random.uniform(0.5, 1.6, (K, 1))).astype(np.float32),
        "gd": (np.random.uniform(0.5, 1.6, (K, 1))).astype(np.float32),
        "wt_words": wtp[0],
        "wt_scales": wtp[1],
        "sa": (np.random.uniform(0.5, 1.6, (R, 1))).astype(np.float32),
        "sb": (np.random.uniform(0.5, 1.6, (R, 1))).astype(np.float32),
        "sd": (np.random.uniform(0.5, 1.6, (R, 1))).astype(np.float32),
        "wb_words": wbp[0],
        "wb_scales": wbp[1],
        "offs": striped8(idx),
        "offs2": striped(idx2),
        "offs3": striped8(idx3),
        "offs4": striped(idx4),
        "offs5": striped8(idx5),
        "offs6": striped8(idx6),
        "offs7": striped(idx7),
    }


def reference(ta, ga, gb, gd, wt_words, wt_scales, sa, sb, sd, wb_words, wb_scales, offs, offs2, offs3, offs4, offs5, offs6, offs7):
    idx = unstriped8(offs)
    idx2 = unstriped(offs2)
    idx3 = unstriped8(offs3)
    idx4 = unstriped(offs4)
    idx5 = unstriped8(offs5)
    idx6 = unstriped8(offs6)
    idx7 = unstriped(offs7)
    wtu = unpack_weight(wt_words, wt_scales, "e2m1")
    wbu = unpack_weight(wb_words, wb_scales, "e4m3")
    xcd = pick8(f64(ta), idx, 64) * f64(ga)
    xc = np.maximum(xcd[:, idx2] * f64(gb), pick8(xcd, idx3, 64) * f64(gd))
    wtidx4g = wtu[:, idx4]
    xcq = mxq(xc, 0, "e4m3")
    a = wtidx4g.T @ xcq
    h1 = pick8(a, idx5, 64) * f64(sa)
    hid = np.abs(pick8(h1, idx6, 64) * f64(sb) - h1[:, idx7] * f64(sd))
    hidq = mxq(hid, 0, "e4m3")
    y = wbu.T @ hidq
    return y

@@ -1,0 +1,207 @@
+from contextlib import ExitStack
+
+import concourse.mybir as mybir
+
+K, J, R, T, U, F, O, S, N = 512, 512, 512, 2048, 1024, 1024, 128, 256, 256
+FLOPS = 2 * K * R * J + 2 * R * N * O
+
+F32 = mybir.dt.float32
+BF16 = mybir.dt.bfloat16
+I32 = mybir.dt.int32
+U32 = mybir.dt.uint32
+U16 = mybir.dt.uint16
+U8 = mybir.dt.uint8
+FP8X4 = mybir.dt.float8_e4m3fn_x4
+FP4X4 = mybir.dt.float4_e2m1fn_x4
+ACT = mybir.ActivationFunctionType
+ALU = mybir.AluOpType
+
+P = 128
+PACK = 4
+CH = 128
+CHUNKS = J // CH
+EARLY = (CHUNKS - 1) * CH
+SPLIT = 3
+
+
+def tile_picked_crossspelled_store_one_chain_one_plain_kernel(
+    tc, ta, ga, gb, gd, wt_words, wt_scales, sa, sb, sd, wb_words, wb_scales,
+    offs, offs2, offs3, offs4, offs5, offs6, offs7, out,
+):
+    nc = tc.nc
+    with ExitStack() as ctx:
+        keep = ctx.enter_context(tc.tile_pool(name="keep", bufs=1))
+        share = ctx.enter_context(tc.tile_pool(name="share", bufs=1))
+        psum = ctx.enter_context(tc.psum_pool(name="psum", bufs=1))
+
+        def load_list(src, name):
+            tile = keep.tile([P, src.shape[1]], U16, name=name)
+            nc.sync.dma_start(tile[:], src)
+            return tile
+
+        def load_factor(src, name, queue, offset=None):
+            if offset is None:
+                tile = keep.tile([P, PACK], F32, name=name)
+            else:
+                tile = share.tile([P, PACK], F32, name=name, offset=offset)
+            queue.dma_start(tile[:], src.rearrange("(p t) o -> p (t o)", t=PACK))
+            return tile
+
+        def load_table(t):
+            if t == PACK - 1:
+                tile = share.tile([P, T], F32, name="ta%d" % t, offset=0)
+            else:
+                tile = keep.tile([P, T], F32, name="ta%d" % t)
+            nc.sync.dma_start(tile[:], ta.rearrange("(p t) c -> p t c", t=PACK)[:, t, :])
+            return tile
+
+        def load_scale_rows(src, width, name):
+            tile = keep.tile([PACK, 4, width // 4], I32, name=name)
+            nc.sync.dma_start(tile[:], src[0].bitcast(I32).rearrange("(q r) c -> r q c", r=4))
+            return tile
+
+        def spread_scale_rows(rows, width, name):
+            tile = keep.tile([P, width], U8, name=name, align_bytes=64)
+            nc.vector.memset(tile[:].bitcast(I32), 0)
+            for q in range(4):
+                nc.vector.tensor_copy(tile[32 * q : 32 * q + 4, :].bitcast(I32), rows[:, q, :])
+            return tile
+
+        def fetch(dst, window, offsets, factor, t):
+            nc.scalar.activation(dst, window[:].indirect(offsets), ACT.Copy, scale=factor[:, t : t + 1])
+
+        ga_sb = load_factor(ga, "ga_sb", nc.scalar)
+        l1 = load_list(offs, "l1")
+        tab = [load_table(0), load_table(1)]
+        l3 = load_list(offs3, "l3")
+        gd_sb = load_factor(gd, "gd_sb", nc.sync, T * 4)
+        l4 = load_list(offs4, "l4")
+        wt_w = keep.tile([P, F], U16, name="wt_w")
+        nc.sync.dma_start(wt_w[:].bitcast(I32), wt_words[0].bitcast(I32))
+        wt_rows = load_scale_rows(wt_scales, F, "wt_rows")
+        tab.append(load_table(2))
+        tab.append(load_table(3))
+        l2 = load_list(offs2, "l2")
+        gb_sb = load_factor(gb, "gb_sb", nc.sync)
+        l5 = load_list(offs5, "l5")
+        sa_sb = load_factor(sa, "sa_sb", nc.sync)
+        l6 = load_list(offs6, "l6")
+        sb_sb = load_factor(sb, "sb_sb", nc.sync)
+        l7 = load_list(offs7, "l7")
+        sd_sb = load_factor(sd, "sd_sb", nc.sync)
+        wb_w = keep.tile([P, N], U32, name="wb_w", align_bytes=64)
+        nc.sync.dma_start(wb_w[:].bitcast(I32), wb_words[0].rearrange("p n t -> p (n t)").bitcast(I32))
+        wb_rows = load_scale_rows(wb_scales, N, "wb_rows")
+
+        wt_s = spread_scale_rows(wt_rows, F, "wt_s")
+        got_w = keep.tile([P, R], U16, name="got_w")
+        nc.vector.tensor_copy(got_w[:], wt_w[:].indirect(l4[:]))
+        got_s = keep.tile([P, R], U8, name="got_s")
+        nc.vector.tensor_copy(got_s[:], wt_s[:].indirect(l4[:]))
+        w1 = keep.tile([P, PACK, P, 2], U8, name="w1", align_bytes=64)
+        nc.vector.tensor_copy(w1[:], got_w[:].bitcast(U8).rearrange("p (m t b) -> p t m b", t=PACK, b=2))
+        s1 = keep.tile([P, PACK, P], U8, name="s1", align_bytes=64)
+        nc.vector.tensor_copy(s1[:], got_s[:].rearrange("p (m t) -> p t m", t=PACK))
+        wb_s = spread_scale_rows(wb_rows, N, "wb_s")
+
+        xcd = [keep.tile([P, U], F32, name="xcd%d" % t) for t in range(PACK)]
+        g3 = keep.tile([P, PACK, J], F32, name="g3")
+        g2_first = share.tile([P, PACK, CH], F32, name="g2_first", offset=0)
+        g2_rest = share.tile([P, CHUNKS - 1, PACK, CH], F32, name="g2_rest", offset=T * 4)
+        g2 = [g2_first[:]] + [g2_rest[:, c] for c in range(CHUNKS - 1)]
+
+        def fetch_g2(c, t):
+            fetch(g2[c][:, t, :], xcd[t], l2[:, c * CH // 16 : (c + 1) * CH // 16], gb_sb, t)
+
+        fetch(xcd[0][:], tab[0], l1[:], ga_sb, 0)
+        fetch(xcd[1][:], tab[1], l1[:], ga_sb, 1)
+        fetch(g3[:, 0, :], xcd[0], l3[:], gd_sb, 0)
+        fetch(g3[:, 1, :], xcd[1], l3[:], gd_sb, 1)
+        fetch(xcd[2][:], tab[2], l1[:], ga_sb, 2)
+        fetch(g3[:, 2, :], xcd[2], l3[:], gd_sb, 2)
+        fetch(xcd[3][:], tab[3], l1[:], ga_sb, 3)
+        for t in range(PACK - 1):
+            fetch_g2(0, t)
+        fetch(g3[:, 3, :], xcd[3], l3[:], gd_sb, 3)
+        fetch_g2(0, 3)
+
+        a_ps = [psum.tile([P, J], F32, name="a_ps%d" % t, tag="bank%d" % t) for t in range(PACK)]
+        last_ps = [psum.tile([P, CH], F32, name="last_ps%d" % t) for t in range(SPLIT)]
+        for c in range(CHUNKS):
+            cols = slice(c * CH, (c + 1) * CH)
+            if c > 0:
+                for t in range(PACK):
+                    fetch_g2(c, t)
+            xb = keep.tile([P, CH, PACK], BF16, name="xb%d" % c, align_bytes=64)
+            nc.vector.tensor_tensor(
+                xb[:].rearrange("p (c i) t -> p c t i", i=4),
+                g2[c].rearrange("p t (c i) -> p c t i", i=4),
+                g3[:, :, cols].rearrange("p t (c i) -> p c t i", i=4),
+                ALU.max,
+            )
+            xq = keep.tile([P, CH], U32, name="xq%d" % c, align_bytes=64)
+            xs = keep.tile([P, CH], U8, name="xs%d" % c, align_bytes=64)
+            nc.vector.quantize_mx(xq[:].bitcast(FP8X4), xs[:], xb[:].rearrange("p c t -> p (c t)"))
+            for t in range(PACK):
+                dst = last_ps[t][:] if c == CHUNKS - 1 and t < SPLIT else a_ps[t][:, cols]
+                nc.tensor.matmul_mx(
+                    dst,
+                    lhsT=w1[:, t].rearrange("p m b -> p (m b)").bitcast(FP4X4),
+                    lhsT_scale=s1[:, t, :],
+                    rhs=xq[:].bitcast(FP8X4),
+                    rhs_scale=xs[:],
+                    start=True,
+                    stop=True,
+                )
+
+        a = [keep.tile([P, J], F32, name="a%d" % t) for t in range(PACK)]
+        for t in range(SPLIT):
+            nc.scalar.activation(a[t][:, :EARLY], a_ps[t][:, :EARLY], ACT.Copy)
+            nc.vector.tensor_copy(a[t][:, EARLY:], last_ps[t][:])
+        for t in range(SPLIT, PACK):
+            nc.vector.tensor_copy(a[t][:], a_ps[t][:])
+
+        h1 = [keep.tile([P, S], F32, name="h1_%d" % t) for t in range(PACK)]
+        diff = keep.tile([P, PACK, O], F32, name="diff")
+
+        def fetch_h1(t):
+            fetch(h1[t][:], a[t], l5[:], sa_sb, t)
+
+        def look_twice(t):
+            g6 = keep.tile([P, O], F32, name="g6_%d" % t)
+            g7 = keep.tile([P, O], F32, name="g7_%d" % t)
+            fetch(g6[:], h1[t], l6[:], sb_sb, t)
+            fetch(g7[:], h1[t], l7[:], sd_sb, t)
+            nc.vector.tensor_tensor(diff[:, t, :], g6[:], g7[:], ALU.subtract)
+
+        fetch_h1(0)
+        for t in range(PACK):
+            if t + 1 < PACK:
+                fetch_h1(t + 1)
+            look_twice(t)
+
+        hb = keep.tile([P, O, PACK], BF16, name="hb", align_bytes=64)
+        woven = diff[:].rearrange("p t c -> p c t")
+        nc.vector.scalar_tensor_tensor(hb[:], woven, -1.0, woven, ALU.mult, ALU.max)
+        hq = keep.tile([P, O], U32, name="hq", align_bytes=64)
+        hs = keep.tile([P, O], U8, name="hs", align_bytes=64)
+        nc.vector.quantize_mx(hq[:].bitcast(FP8X4), hs[:], hb[:].rearrange("p c t -> p (c t)"))
+        for h in range(N // P):
+            rows = slice(h * P, (h + 1) * P)
+            y_ps = psum.tile([P, O], F32, name="y_ps%d" % h, tag="bank%d" % h)
+            nc.tensor.matmul_mx(
+                y_ps[:],
+                lhsT=wb_w[:, rows].bitcast(FP8X4),
+                lhsT_scale=wb_s[:, rows],
+                rhs=hq[:].bitcast(FP8X4),
+                rhs_scale=hs[:],
+                start=True,
+                stop=True,
+            )
+            y = keep.tile([P, O], F32, name="y%d" % h)
+            if h == 0:
+                nc.vector.tensor_copy(y[:], y_ps[:])
+                nc.sync.dma_start(out[rows, :], y[:])
+            else:
+                nc.scalar.activation(y[:], y_ps[:], ACT.Copy)
+                nc.scalar.dma_start(out[rows, :], y[:])

@@ -21,7 +21,7 @@ PACK = 4
 CH = 128
 CHUNKS = J // CH
 EARLY = (CHUNKS - 1) * CH
-SPLIT = 3
+SPLIT = 2
 
 
 def tile_picked_crossspelled_store_one_chain_one_plain_kernel(
@@ -31,7 +31,6 @@ def tile_picked_crossspelled_store_one_chain_one_plain_kernel(
     nc = tc.nc
     with ExitStack() as ctx:
         keep = ctx.enter_context(tc.tile_pool(name="keep", bufs=1))
-        share = ctx.enter_context(tc.tile_pool(name="share", bufs=1))
         psum = ctx.enter_context(tc.psum_pool(name="psum", bufs=1))
 
         def load_list(src, name):
@@ -39,19 +38,13 @@ def tile_picked_crossspelled_store_one_chain_one_plain_kernel(
             nc.sync.dma_start(tile[:], src)
             return tile
 
-        def load_factor(src, name, queue, offset=None):
-            if offset is None:
-                tile = keep.tile([P, PACK], F32, name=name)
-            else:
-                tile = share.tile([P, PACK], F32, name=name, offset=offset)
+        def load_factor(src, name, queue):
+            tile = keep.tile([P, PACK], F32, name=name)
             queue.dma_start(tile[:], src.rearrange("(p t) o -> p (t o)", t=PACK))
             return tile
 
         def load_table(t):
-            if t == PACK - 1:
-                tile = share.tile([P, T], F32, name="ta%d" % t, offset=0)
-            else:
-                tile = keep.tile([P, T], F32, name="ta%d" % t)
+            tile = keep.tile([P, T], F32, name="ta%d" % t)
             nc.sync.dma_start(tile[:], ta.rearrange("(p t) c -> p t c", t=PACK)[:, t, :])
             return tile
 
@@ -71,18 +64,19 @@ def tile_picked_crossspelled_store_one_chain_one_plain_kernel(
             nc.scalar.activation(dst, window[:].indirect(offsets), ACT.Copy, scale=factor[:, t : t + 1])
 
         ga_sb = load_factor(ga, "ga_sb", nc.scalar)
+        tab = [load_table(0)]
         l1 = load_list(offs, "l1")
-        tab = [load_table(0), load_table(1)]
-        l3 = load_list(offs3, "l3")
-        gd_sb = load_factor(gd, "gd_sb", nc.sync, T * 4)
+        tab.append(load_table(1))
+        tab.append(load_table(2))
+        l2 = load_list(offs2, "l2")
+        gb_sb = load_factor(gb, "gb_sb", nc.sync)
         l4 = load_list(offs4, "l4")
         wt_w = keep.tile([P, F], U16, name="wt_w")
         nc.sync.dma_start(wt_w[:].bitcast(I32), wt_words[0].bitcast(I32))
-        wt_rows = load_scale_rows(wt_scales, F, "wt_rows")
-        tab.append(load_table(2))
         tab.append(load_table(3))
-        l2 = load_list(offs2, "l2")
-        gb_sb = load_factor(gb, "gb_sb", nc.sync)
+        wt_rows = load_scale_rows(wt_scales, F, "wt_rows")
+        l3 = load_list(offs3, "l3")
+        gd_sb = load_factor(gd, "gd_sb", nc.sync)
         l5 = load_list(offs5, "l5")
         sa_sb = load_factor(sa, "sa_sb", nc.sync)
         l6 = load_list(offs6, "l6")
@@ -105,43 +99,47 @@ def tile_picked_crossspelled_store_one_chain_one_plain_kernel(
         wb_s = spread_scale_rows(wb_rows, N, "wb_s")
 
         xcd = [keep.tile([P, U], F32, name="xcd%d" % t) for t in range(PACK)]
-        g3 = keep.tile([P, PACK, J], F32, name="g3")
-        g2_first = share.tile([P, PACK, CH], F32, name="g2_first", offset=0)
-        g2_rest = share.tile([P, CHUNKS - 1, PACK, CH], F32, name="g2_rest", offset=T * 4)
-        g2 = [g2_first[:]] + [g2_rest[:, c] for c in range(CHUNKS - 1)]
 
-        def fetch_g2(c, t):
-            fetch(g2[c][:, t, :], xcd[t], l2[:, c * CH // 16 : (c + 1) * CH // 16], gb_sb, t)
-
-        fetch(xcd[0][:], tab[0], l1[:], ga_sb, 0)
-        fetch(xcd[1][:], tab[1], l1[:], ga_sb, 1)
-        fetch(g3[:, 0, :], xcd[0], l3[:], gd_sb, 0)
-        fetch(g3[:, 1, :], xcd[1], l3[:], gd_sb, 1)
-        fetch(xcd[2][:], tab[2], l1[:], ga_sb, 2)
-        fetch(g3[:, 2, :], xcd[2], l3[:], gd_sb, 2)
-        fetch(xcd[3][:], tab[3], l1[:], ga_sb, 3)
         for t in range(PACK - 1):
-            fetch_g2(0, t)
-        fetch(g3[:, 3, :], xcd[3], l3[:], gd_sb, 3)
-        fetch_g2(0, 3)
+            fetch(xcd[t][:], tab[t], l1[:], ga_sb, t)
+        g2_first = keep.tile([P, PACK, CH], F32, name="g2_first", tag="ta2")
+
+        def fetch_g2(dst, start, width, t):
+            fetch(dst, xcd[t], l2[:, start // 16 : (start + width) // 16], gb_sb, t)
+
+        for t in range(PACK - 1):
+            fetch_g2(g2_first[:, t, :], 0, CH, t)
+        fetch(xcd[3][:], tab[3], l1[:], ga_sb, 3)
+        g3 = keep.tile([P, PACK, J], F32, name="g3", tag="ta3")
+        for t in range(PACK):
+            fetch(g3[:, t, :], xcd[t], l3[:], gd_sb, t)
+        fetch_g2(g2_first[:, 3, :], 0, CH, 3)
+        g2_rest = keep.tile([P, PACK * EARLY], F32, name="g2_rest", tag="gd_sb")
 
         a_ps = [psum.tile([P, J], F32, name="a_ps%d" % t, tag="bank%d" % t) for t in range(PACK)]
         last_ps = [psum.tile([P, CH], F32, name="last_ps%d" % t) for t in range(SPLIT)]
         for c in range(CHUNKS):
             cols = slice(c * CH, (c + 1) * CH)
-            if c > 0:
-                for t in range(PACK):
-                    fetch_g2(c, t)
-            xb = keep.tile([P, CH, PACK], BF16, name="xb%d" % c, align_bytes=64)
-            nc.vector.tensor_tensor(
-                xb[:].rearrange("p (c i) t -> p c t i", i=4),
-                g2[c].rearrange("p t (c i) -> p c t i", i=4),
-                g3[:, :, cols].rearrange("p t (c i) -> p c t i", i=4),
-                ALU.max,
-            )
             xq = keep.tile([P, CH], U32, name="xq%d" % c, align_bytes=64)
             xs = keep.tile([P, CH], U8, name="xs%d" % c, align_bytes=64)
-            nc.vector.quantize_mx(xq[:].bitcast(FP8X4), xs[:], xb[:].rearrange("p c t -> p (c t)"))
+            width = CH if c < CHUNKS - 1 else CH // 2
+            for start in range(c * CH, (c + 1) * CH, width):
+                if c == 0:
+                    g2 = g2_first[:]
+                else:
+                    at = PACK * (start - CH)
+                    g2 = g2_rest[:, at : at + PACK * width].rearrange("p (t c) -> p t c", t=PACK)
+                    for t in range(PACK):
+                        fetch_g2(g2[:, t, :], start, width, t)
+                xb = keep.tile([P, width, PACK], BF16, name="xb", align_bytes=64, bufs=2)
+                nc.vector.tensor_tensor(
+                    xb[:].rearrange("p (c i) t -> p c t i", i=4),
+                    g2.rearrange("p t (c i) -> p c t i", i=4),
+                    g3[:, :, start : start + width].rearrange("p t (c i) -> p c t i", i=4),
+                    ALU.max,
+                )
+                part = slice(start - c * CH, start - c * CH + width)
+                nc.vector.quantize_mx(xq[:, part].bitcast(FP8X4), xs[:, part], xb[:].rearrange("p c t -> p (c t)"))
             for t in range(PACK):
                 dst = last_ps[t][:] if c == CHUNKS - 1 and t < SPLIT else a_ps[t][:, cols]
                 nc.tensor.matmul_mx(
@@ -168,11 +166,10 @@ def tile_picked_crossspelled_store_one_chain_one_plain_kernel(
             fetch(h1[t][:], a[t], l5[:], sa_sb, t)
 
         def look_twice(t):
-            g6 = keep.tile([P, O], F32, name="g6_%d" % t)
-            g7 = keep.tile([P, O], F32, name="g7_%d" % t)
-            fetch(g6[:], h1[t], l6[:], sb_sb, t)
-            fetch(g7[:], h1[t], l7[:], sd_sb, t)
-            nc.vector.tensor_tensor(diff[:, t, :], g6[:], g7[:], ALU.subtract)
+            looks = keep.tile([P, 2, O], F32, name="looks%d" % t, tag="a%d" % (t + 1))
+            fetch(looks[:, 0, :], h1[t], l6[:], sb_sb, t)
+            fetch(looks[:, 1, :], h1[t], l7[:], sd_sb, t)
+            nc.vector.tensor_tensor(diff[:, t, :], looks[:, 0, :], looks[:, 1, :], ALU.subtract)
 
         fetch_h1(0)
         for t in range(PACK):
@@ -181,8 +178,11 @@ def tile_picked_crossspelled_store_one_chain_one_plain_kernel(
             look_twice(t)
 
         hb = keep.tile([P, O, PACK], BF16, name="hb", align_bytes=64)
-        woven = diff[:].rearrange("p t c -> p c t")
-        nc.vector.scalar_tensor_tensor(hb[:], woven, -1.0, woven, ALU.mult, ALU.max)
+        nc.scalar.activation(
+            hb[:].rearrange("p (c i) t -> p c t i", i=4),
+            diff[:].rearrange("p t (c i) -> p c t i", i=4),
+            ACT.Abs,
+        )
         hq = keep.tile([P, O], U32, name="hq", align_bytes=64)
         hs = keep.tile([P, O], U8, name="hs", align_bytes=64)
         nc.vector.quantize_mx(hq[:].bitcast(FP8X4), hs[:], hb[:].rearrange("p c t -> p (c t)"))

@@ -22,6 +22,7 @@ CH = 128
 CHUNKS = J // CH
 EARLY = (CHUNKS - 1) * CH
 SPLIT = 2
+FIRST = J // 2
 
 
 def tile_picked_crossspelled_store_one_chain_one_plain_kernel(
@@ -102,46 +103,45 @@ def tile_picked_crossspelled_store_one_chain_one_plain_kernel(
 
         for t in range(PACK - 1):
             fetch(xcd[t][:], tab[t], l1[:], ga_sb, t)
-        g2_first = keep.tile([P, PACK, CH], F32, name="g2_first", tag="ta2")
+        g2_first = keep.tile([P, PACK, FIRST], F32, name="g2_first", tag="ta2")
 
         def fetch_g2(dst, start, width, t):
             fetch(dst, xcd[t], l2[:, start // 16 : (start + width) // 16], gb_sb, t)
 
         for t in range(PACK - 1):
-            fetch_g2(g2_first[:, t, :], 0, CH, t)
+            fetch_g2(g2_first[:, t, :], 0, FIRST, t)
         fetch(xcd[3][:], tab[3], l1[:], ga_sb, 3)
         g3 = keep.tile([P, PACK, J], F32, name="g3", tag="ta3")
-        for t in range(PACK):
+        for t in range(PACK - 1):
             fetch(g3[:, t, :], xcd[t], l3[:], gd_sb, t)
-        fetch_g2(g2_first[:, 3, :], 0, CH, 3)
-        g2_rest = keep.tile([P, PACK * EARLY], F32, name="g2_rest", tag="gd_sb")
+        fetch(g3[:, 3, :FIRST], xcd[3], l3[:, : FIRST // 16], gd_sb, 3)
+        fetch_g2(g2_first[:, 3, :], 0, FIRST, 3)
+        fetch(g3[:, 3, FIRST:], xcd[3], l3[:, FIRST // 16 :], gd_sb, 3)
+        g2_rest = keep.tile([P, PACK * (J - FIRST)], F32, name="g2_rest", tag="gd_sb")
 
         a_ps = [psum.tile([P, J], F32, name="a_ps%d" % t, tag="bank%d" % t) for t in range(PACK)]
         last_ps = [psum.tile([P, CH], F32, name="last_ps%d" % t) for t in range(SPLIT)]
-        for c in range(CHUNKS):
-            cols = slice(c * CH, (c + 1) * CH)
-            xq = keep.tile([P, CH], U32, name="xq%d" % c, align_bytes=64)
-            xs = keep.tile([P, CH], U8, name="xs%d" % c, align_bytes=64)
-            width = CH if c < CHUNKS - 1 else CH // 2
-            for start in range(c * CH, (c + 1) * CH, width):
-                if c == 0:
-                    g2 = g2_first[:]
-                else:
-                    at = PACK * (start - CH)
-                    g2 = g2_rest[:, at : at + PACK * width].rearrange("p (t c) -> p t c", t=PACK)
-                    for t in range(PACK):
-                        fetch_g2(g2[:, t, :], start, width, t)
-                xb = keep.tile([P, width, PACK], BF16, name="xb", align_bytes=64, bufs=2)
-                nc.vector.tensor_tensor(
-                    xb[:].rearrange("p (c i) t -> p c t i", i=4),
-                    g2.rearrange("p t (c i) -> p c t i", i=4),
-                    g3[:, :, start : start + width].rearrange("p t (c i) -> p c t i", i=4),
-                    ALU.max,
-                )
-                part = slice(start - c * CH, start - c * CH + width)
-                nc.vector.quantize_mx(xq[:, part].bitcast(FP8X4), xs[:, part], xb[:].rearrange("p c t -> p (c t)"))
+        for start, width in ((0, FIRST), (FIRST, CH), (EARLY, CH)):
+            cols = slice(start, start + width)
+            if start == 0:
+                g2 = g2_first[:]
+            else:
+                at = PACK * (start - FIRST)
+                g2 = g2_rest[:, at : at + PACK * width].rearrange("p (t c) -> p t c", t=PACK)
+                for t in range(PACK):
+                    fetch_g2(g2[:, t, :], start, width, t)
+            xb = keep.tile([P, width, PACK], BF16, name="xb", align_bytes=64)
+            nc.vector.tensor_tensor(
+                xb[:].rearrange("p (c i) t -> p c t i", i=4),
+                g2.rearrange("p t (c i) -> p c t i", i=4),
+                g3[:, :, cols].rearrange("p t (c i) -> p c t i", i=4),
+                ALU.max,
+            )
+            xq = keep.tile([P, width], U32, name="xq%d" % start, align_bytes=64)
+            xs = keep.tile([P, width], U8, name="xs%d" % start, align_bytes=64)
+            nc.vector.quantize_mx(xq[:].bitcast(FP8X4), xs[:], xb[:].rearrange("p c t -> p (c t)"))
             for t in range(PACK):
-                dst = last_ps[t][:] if c == CHUNKS - 1 and t < SPLIT else a_ps[t][:, cols]
+                dst = last_ps[t][:] if start == EARLY and t < SPLIT else a_ps[t][:, cols]
                 nc.tensor.matmul_mx(
                     dst,
                     lhsT=w1[:, t].rearrange("p m b -> p (m b)").bitcast(FP4X4),

@@ -65,6 +65,9 @@ def tile_picked_crossspelled_store_one_chain_one_plain_kernel(
             nc.scalar.activation(dst, window[:].indirect(offsets), ACT.Copy, scale=factor[:, t : t + 1])
 
         ga_sb = load_factor(ga, "ga_sb", nc.scalar)
+        warm = keep.tile([P, 16], F32, name="warm")
+        nc.vector.memset(warm[:, 0:1], 0.0)
+        nc.scalar.activation(warm[:, 8:9], warm[:, 0:1], ACT.Copy)
         tab = [load_table(0)]
         l1 = load_list(offs, "l1")
         tab.append(load_table(1))

@@ -18,11 +18,16 @@ ALU = mybir.AluOpType
 
 P = 128
 PACK = 4
-CH = 128
-CHUNKS = J // CH
-EARLY = (CHUNKS - 1) * CH
-SPLIT = 2
+LAST = PACK - 1
+GROUP = 16
+QUADS = 4
+LINE = 4
+
 FIRST = J // 2
+NARROW = 128
+EARLY = J - NARROW
+SCALAR_TILES = 2
+HALF = O // 2
 
 
 def tile_picked_crossspelled_store_one_chain_one_plain_kernel(
@@ -50,19 +55,28 @@ def tile_picked_crossspelled_store_one_chain_one_plain_kernel(
             return tile
 
         def load_scale_rows(src, width, name):
-            tile = keep.tile([PACK, 4, width // 4], I32, name=name)
-            nc.sync.dma_start(tile[:], src[0].bitcast(I32).rearrange("(q r) c -> r q c", r=4))
+            tile = keep.tile([4, QUADS, width // 4], I32, name=name)
+            nc.sync.dma_start(tile[:], src[0].bitcast(I32).rearrange("(q i) c -> i q c", q=QUADS))
             return tile
 
-        def spread_scale_rows(rows, width, name):
+        def spread_scale_rows(staged, width, name):
             tile = keep.tile([P, width], U8, name=name, align_bytes=64)
             nc.vector.memset(tile[:].bitcast(I32), 0)
-            for q in range(4):
-                nc.vector.tensor_copy(tile[32 * q : 32 * q + 4, :].bitcast(I32), rows[:, q, :])
+            for q in range(QUADS):
+                nc.vector.tensor_copy(tile[32 * q : 32 * q + 4, :].bitcast(I32), staged[:, q, :])
             return tile
 
         def fetch(dst, window, offsets, factor, t):
             nc.scalar.activation(dst, window[:].indirect(offsets), ACT.Copy, scale=factor[:, t : t + 1])
+
+        def entries(lst, start, count):
+            return lst[:, start // GROUP : (start + count) // GROUP]
+
+        def by_lines(planes):
+            return planes.rearrange("p t (c i) -> p c t i", i=LINE)
+
+        def woven_by_lines(words):
+            return words.rearrange("p (c i) t -> p c t i", i=LINE)
 
         ga_sb = load_factor(ga, "ga_sb", nc.scalar)
         warm = keep.tile([P, 16], F32, name="warm")
@@ -77,7 +91,7 @@ def tile_picked_crossspelled_store_one_chain_one_plain_kernel(
         l4 = load_list(offs4, "l4")
         wt_w = keep.tile([P, F], U16, name="wt_w")
         nc.sync.dma_start(wt_w[:].bitcast(I32), wt_words[0].bitcast(I32))
-        tab.append(load_table(3))
+        tab.append(load_table(LAST))
         wt_rows = load_scale_rows(wt_scales, F, "wt_rows")
         l3 = load_list(offs3, "l3")
         gd_sb = load_factor(gd, "gd_sb", nc.sync)
@@ -103,28 +117,27 @@ def tile_picked_crossspelled_store_one_chain_one_plain_kernel(
         wb_s = spread_scale_rows(wb_rows, N, "wb_s")
 
         xcd = [keep.tile([P, U], F32, name="xcd%d" % t) for t in range(PACK)]
-
-        for t in range(PACK - 1):
+        for t in range(LAST):
             fetch(xcd[t][:], tab[t], l1[:], ga_sb, t)
         g2_first = keep.tile([P, PACK, FIRST], F32, name="g2_first", tag="ta2")
 
         def fetch_g2(dst, start, width, t):
-            fetch(dst, xcd[t], l2[:, start // 16 : (start + width) // 16], gb_sb, t)
+            fetch(dst, xcd[t], entries(l2, start, width), gb_sb, t)
 
-        for t in range(PACK - 1):
+        for t in range(LAST):
             fetch_g2(g2_first[:, t, :], 0, FIRST, t)
-        fetch(xcd[3][:], tab[3], l1[:], ga_sb, 3)
+        fetch(xcd[LAST][:], tab[LAST], l1[:], ga_sb, LAST)
         g3 = keep.tile([P, PACK, J], F32, name="g3", tag="ta3")
-        for t in range(PACK - 1):
+        for t in range(LAST):
             fetch(g3[:, t, :], xcd[t], l3[:], gd_sb, t)
-        fetch(g3[:, 3, :FIRST], xcd[3], l3[:, : FIRST // 16], gd_sb, 3)
-        fetch_g2(g2_first[:, 3, :], 0, FIRST, 3)
-        fetch(g3[:, 3, FIRST:], xcd[3], l3[:, FIRST // 16 :], gd_sb, 3)
+        fetch(g3[:, LAST, :FIRST], xcd[LAST], entries(l3, 0, FIRST), gd_sb, LAST)
+        fetch_g2(g2_first[:, LAST, :], 0, FIRST, LAST)
+        fetch(g3[:, LAST, FIRST:], xcd[LAST], entries(l3, FIRST, J - FIRST), gd_sb, LAST)
         g2_rest = keep.tile([P, PACK * (J - FIRST)], F32, name="g2_rest", tag="gd_sb")
 
         a_ps = [psum.tile([P, J], F32, name="a_ps%d" % t, tag="bank%d" % t) for t in range(PACK)]
-        last_ps = [psum.tile([P, CH], F32, name="last_ps%d" % t) for t in range(SPLIT)]
-        for start, width in ((0, FIRST), (FIRST, CH), (EARLY, CH)):
+        last_ps = [psum.tile([P, NARROW], F32, name="last_ps%d" % t) for t in range(SCALAR_TILES)]
+        for start, width in ((0, FIRST), (FIRST, NARROW), (EARLY, NARROW)):
             cols = slice(start, start + width)
             if start == 0:
                 g2 = g2_first[:]
@@ -134,17 +147,12 @@ def tile_picked_crossspelled_store_one_chain_one_plain_kernel(
                 for t in range(PACK):
                     fetch_g2(g2[:, t, :], start, width, t)
             xb = keep.tile([P, width, PACK], BF16, name="xb", align_bytes=64)
-            nc.vector.tensor_tensor(
-                xb[:].rearrange("p (c i) t -> p c t i", i=4),
-                g2.rearrange("p t (c i) -> p c t i", i=4),
-                g3[:, :, cols].rearrange("p t (c i) -> p c t i", i=4),
-                ALU.max,
-            )
+            nc.vector.tensor_tensor(woven_by_lines(xb[:]), by_lines(g2), by_lines(g3[:, :, cols]), ALU.max)
             xq = keep.tile([P, width], U32, name="xq%d" % start, align_bytes=64)
             xs = keep.tile([P, width], U8, name="xs%d" % start, align_bytes=64)
             nc.vector.quantize_mx(xq[:].bitcast(FP8X4), xs[:], xb[:].rearrange("p c t -> p (c t)"))
             for t in range(PACK):
-                dst = last_ps[t][:] if start == EARLY and t < SPLIT else a_ps[t][:, cols]
+                dst = last_ps[t][:] if start == EARLY and t < SCALAR_TILES else a_ps[t][:, cols]
                 nc.tensor.matmul_mx(
                     dst,
                     lhsT=w1[:, t].rearrange("p m b -> p (m b)").bitcast(FP4X4),
@@ -156,10 +164,10 @@ def tile_picked_crossspelled_store_one_chain_one_plain_kernel(
                 )
 
         a = [keep.tile([P, J], F32, name="a%d" % t) for t in range(PACK)]
-        for t in range(SPLIT):
+        for t in range(SCALAR_TILES):
             nc.scalar.activation(a[t][:, :EARLY], a_ps[t][:, :EARLY], ACT.Copy)
             nc.vector.tensor_copy(a[t][:, EARLY:], last_ps[t][:])
-        for t in range(SPLIT, PACK):
+        for t in range(SCALAR_TILES, PACK):
             nc.vector.tensor_copy(a[t][:], a_ps[t][:])
 
         h1 = [keep.tile([P, S], F32, name="h1_%d" % t) for t in range(PACK)]
@@ -171,24 +179,26 @@ def tile_picked_crossspelled_store_one_chain_one_plain_kernel(
         def look_twice(t):
             looks = keep.tile([P, 2, O], F32, name="looks%d" % t, tag="a%d" % (t + 1))
             fetch(looks[:, 0, :], h1[t], l6[:], sb_sb, t)
-            fetch(looks[:, 1, :], h1[t], l7[:], sd_sb, t)
-            nc.vector.tensor_tensor(diff[:, t, :], looks[:, 0, :], looks[:, 1, :], ALU.subtract)
+            width = O if t < LAST else HALF
+            for at in range(0, O, width):
+                cols = slice(at, at + width)
+                fetch(looks[:, 1, cols], h1[t], entries(l7, at, width), sd_sb, t)
+                nc.vector.tensor_tensor(diff[:, t, cols], looks[:, 0, cols], looks[:, 1, cols], ALU.subtract)
 
         fetch_h1(0)
         for t in range(PACK):
-            if t + 1 < PACK:
+            if t < LAST:
                 fetch_h1(t + 1)
             look_twice(t)
 
         hb = keep.tile([P, O, PACK], BF16, name="hb", align_bytes=64)
-        nc.scalar.activation(
-            hb[:].rearrange("p (c i) t -> p c t i", i=4),
-            diff[:].rearrange("p t (c i) -> p c t i", i=4),
-            ACT.Abs,
-        )
+        by_columns = diff[:, :, :HALF].rearrange("p t c -> p c t")
+        nc.vector.scalar_tensor_tensor(hb[:, :HALF, :], by_columns, -1.0, by_columns, ALU.mult, ALU.max)
+        nc.scalar.activation(woven_by_lines(hb[:, HALF:, :]), by_lines(diff[:, :, HALF:]), ACT.Abs)
         hq = keep.tile([P, O], U32, name="hq", align_bytes=64)
         hs = keep.tile([P, O], U8, name="hs", align_bytes=64)
         nc.vector.quantize_mx(hq[:].bitcast(FP8X4), hs[:], hb[:].rearrange("p c t -> p (c t)"))
+
         for h in range(N // P):
             rows = slice(h * P, (h + 1) * P)
             y_ps = psum.tile([P, O], F32, name="y_ps%d" % h, tag="bank%d" % h)

from contextlib import ExitStack

import concourse.mybir as mybir

K, J, R, T, U, F, O, S, N = 512, 512, 512, 2048, 1024, 1024, 128, 256, 256
FLOPS = 2 * K * R * J + 2 * R * N * O

F32 = mybir.dt.float32
BF16 = mybir.dt.bfloat16
I32 = mybir.dt.int32
U32 = mybir.dt.uint32
U16 = mybir.dt.uint16
U8 = mybir.dt.uint8
FP8X4 = mybir.dt.float8_e4m3fn_x4
FP4X4 = mybir.dt.float4_e2m1fn_x4
ACT = mybir.ActivationFunctionType
ALU = mybir.AluOpType

P = 128
PACK = 4
LAST = PACK - 1
GROUP = 16
QUADS = 4
LINE = 4

FIRST = J // 2
NARROW = 128
EARLY = J - NARROW
SCALAR_TILES = 2
HALF = O // 2


def tile_picked_crossspelled_store_one_chain_one_plain_kernel(
    tc, ta, ga, gb, gd, wt_words, wt_scales, sa, sb, sd, wb_words, wb_scales,
    offs, offs2, offs3, offs4, offs5, offs6, offs7, out,
):
    nc = tc.nc
    with ExitStack() as ctx:
        keep = ctx.enter_context(tc.tile_pool(name="keep", bufs=1))
        psum = ctx.enter_context(tc.psum_pool(name="psum", bufs=1))

        def load_list(src, name):
            tile = keep.tile([P, src.shape[1]], U16, name=name)
            nc.sync.dma_start(tile[:], src)
            return tile

        def load_factor(src, name, queue):
            tile = keep.tile([P, PACK], F32, name=name)
            queue.dma_start(tile[:], src.rearrange("(p t) o -> p (t o)", t=PACK))
            return tile

        def load_table(t):
            tile = keep.tile([P, T], F32, name="ta%d" % t)
            nc.sync.dma_start(tile[:], ta.rearrange("(p t) c -> p t c", t=PACK)[:, t, :])
            return tile

        def load_scale_rows(src, width, name):
            tile = keep.tile([4, QUADS, width // 4], I32, name=name)
            nc.sync.dma_start(tile[:], src[0].bitcast(I32).rearrange("(q i) c -> i q c", q=QUADS))
            return tile

        def spread_scale_rows(staged, width, name):
            tile = keep.tile([P, width], U8, name=name, align_bytes=64)
            nc.vector.memset(tile[:].bitcast(I32), 0)
            for q in range(QUADS):
                nc.vector.tensor_copy(tile[32 * q : 32 * q + 4, :].bitcast(I32), staged[:, q, :])
            return tile

        def fetch(dst, window, offsets, factor, t):
            nc.scalar.activation(dst, window[:].indirect(offsets), ACT.Copy, scale=factor[:, t : t + 1])

        def entries(lst, start, count):
            return lst[:, start // GROUP : (start + count) // GROUP]

        def by_lines(planes):
            return planes.rearrange("p t (c i) -> p c t i", i=LINE)

        def woven_by_lines(words):
            return words.rearrange("p (c i) t -> p c t i", i=LINE)

        ga_sb = load_factor(ga, "ga_sb", nc.scalar)
        warm = keep.tile([P, 16], F32, name="warm")
        nc.vector.memset(warm[:, 0:1], 0.0)
        nc.scalar.activation(warm[:, 8:9], warm[:, 0:1], ACT.Copy)
        tab = [load_table(0)]
        l1 = load_list(offs, "l1")
        tab.append(load_table(1))
        tab.append(load_table(2))
        l2 = load_list(offs2, "l2")
        gb_sb = load_factor(gb, "gb_sb", nc.sync)
        l4 = load_list(offs4, "l4")
        wt_w = keep.tile([P, F], U16, name="wt_w")
        nc.sync.dma_start(wt_w[:].bitcast(I32), wt_words[0].bitcast(I32))
        tab.append(load_table(LAST))
        wt_rows = load_scale_rows(wt_scales, F, "wt_rows")
        l3 = load_list(offs3, "l3")
        gd_sb = load_factor(gd, "gd_sb", nc.sync)
        l5 = load_list(offs5, "l5")
        sa_sb = load_factor(sa, "sa_sb", nc.sync)
        l6 = load_list(offs6, "l6")
        sb_sb = load_factor(sb, "sb_sb", nc.sync)
        l7 = load_list(offs7, "l7")
        sd_sb = load_factor(sd, "sd_sb", nc.sync)
        wb_w = keep.tile([P, N], U32, name="wb_w", align_bytes=64)
        nc.sync.dma_start(wb_w[:].bitcast(I32), wb_words[0].rearrange("p n t -> p (n t)").bitcast(I32))
        wb_rows = load_scale_rows(wb_scales, N, "wb_rows")

        wt_s = spread_scale_rows(wt_rows, F, "wt_s")
        got_w = keep.tile([P, R], U16, name="got_w")
        nc.vector.tensor_copy(got_w[:], wt_w[:].indirect(l4[:]))
        got_s = keep.tile([P, R], U8, name="got_s")
        nc.vector.tensor_copy(got_s[:], wt_s[:].indirect(l4[:]))
        w1 = keep.tile([P, PACK, P, 2], U8, name="w1", align_bytes=64)
        nc.vector.tensor_copy(w1[:], got_w[:].bitcast(U8).rearrange("p (m t b) -> p t m b", t=PACK, b=2))
        s1 = keep.tile([P, PACK, P], U8, name="s1", align_bytes=64)
        nc.vector.tensor_copy(s1[:], got_s[:].rearrange("p (m t) -> p t m", t=PACK))
        wb_s = spread_scale_rows(wb_rows, N, "wb_s")

        xcd = [keep.tile([P, U], F32, name="xcd%d" % t) for t in range(PACK)]
        for t in range(LAST):
            fetch(xcd[t][:], tab[t], l1[:], ga_sb, t)
        g2_first = keep.tile([P, PACK, FIRST], F32, name="g2_first", tag="ta2")

        def fetch_g2(dst, start, width, t):
            fetch(dst, xcd[t], entries(l2, start, width), gb_sb, t)

        for t in range(LAST):
            fetch_g2(g2_first[:, t, :], 0, FIRST, t)
        fetch(xcd[LAST][:], tab[LAST], l1[:], ga_sb, LAST)
        g3 = keep.tile([P, PACK, J], F32, name="g3", tag="ta3")
        for t in range(LAST):
            fetch(g3[:, t, :], xcd[t], l3[:], gd_sb, t)
        fetch(g3[:, LAST, :FIRST], xcd[LAST], entries(l3, 0, FIRST), gd_sb, LAST)
        fetch_g2(g2_first[:, LAST, :], 0, FIRST, LAST)
        fetch(g3[:, LAST, FIRST:], xcd[LAST], entries(l3, FIRST, J - FIRST), gd_sb, LAST)
        g2_rest = keep.tile([P, PACK * (J - FIRST)], F32, name="g2_rest", tag="gd_sb")

        a_ps = [psum.tile([P, J], F32, name="a_ps%d" % t, tag="bank%d" % t) for t in range(PACK)]
        last_ps = [psum.tile([P, NARROW], F32, name="last_ps%d" % t) for t in range(SCALAR_TILES)]
        for start, width in ((0, FIRST), (FIRST, NARROW), (EARLY, NARROW)):
            cols = slice(start, start + width)
            if start == 0:
                g2 = g2_first[:]
            else:
                at = PACK * (start - FIRST)
                g2 = g2_rest[:, at : at + PACK * width].rearrange("p (t c) -> p t c", t=PACK)
                for t in range(PACK):
                    fetch_g2(g2[:, t, :], start, width, t)
            xb = keep.tile([P, width, PACK], BF16, name="xb", align_bytes=64)
            nc.vector.tensor_tensor(woven_by_lines(xb[:]), by_lines(g2), by_lines(g3[:, :, cols]), ALU.max)
            xq = keep.tile([P, width], U32, name="xq%d" % start, align_bytes=64)
            xs = keep.tile([P, width], U8, name="xs%d" % start, align_bytes=64)
            nc.vector.quantize_mx(xq[:].bitcast(FP8X4), xs[:], xb[:].rearrange("p c t -> p (c t)"))
            for t in range(PACK):
                dst = last_ps[t][:] if start == EARLY and t < SCALAR_TILES else a_ps[t][:, cols]
                nc.tensor.matmul_mx(
                    dst,
                    lhsT=w1[:, t].rearrange("p m b -> p (m b)").bitcast(FP4X4),
                    lhsT_scale=s1[:, t, :],
                    rhs=xq[:].bitcast(FP8X4),
                    rhs_scale=xs[:],
                    start=True,
                    stop=True,
                )

        a = [keep.tile([P, J], F32, name="a%d" % t) for t in range(PACK)]
        for t in range(SCALAR_TILES):
            nc.scalar.activation(a[t][:, :EARLY], a_ps[t][:, :EARLY], ACT.Copy)
            nc.vector.tensor_copy(a[t][:, EARLY:], last_ps[t][:])
        for t in range(SCALAR_TILES, PACK):
            nc.vector.tensor_copy(a[t][:], a_ps[t][:])

        h1 = [keep.tile([P, S], F32, name="h1_%d" % t) for t in range(PACK)]
        diff = keep.tile([P, PACK, O], F32, name="diff")

        def fetch_h1(t):
            fetch(h1[t][:], a[t], l5[:], sa_sb, t)

        def look_twice(t):
            looks = keep.tile([P, 2, O], F32, name="looks%d" % t, tag="a%d" % (t + 1))
            fetch(looks[:, 0, :], h1[t], l6[:], sb_sb, t)
            width = O if t < LAST else HALF
            for at in range(0, O, width):
                cols = slice(at, at + width)
                fetch(looks[:, 1, cols], h1[t], entries(l7, at, width), sd_sb, t)
                nc.vector.tensor_tensor(diff[:, t, cols], looks[:, 0, cols], looks[:, 1, cols], ALU.subtract)

        fetch_h1(0)
        for t in range(PACK):
            if t < LAST:
                fetch_h1(t + 1)
            look_twice(t)

        hb = keep.tile([P, O, PACK], BF16, name="hb", align_bytes=64)
        by_columns = diff[:, :, :HALF].rearrange("p t c -> p c t")
        nc.vector.scalar_tensor_tensor(hb[:, :HALF, :], by_columns, -1.0, by_columns, ALU.mult, ALU.max)
        nc.scalar.activation(woven_by_lines(hb[:, HALF:, :]), by_lines(diff[:, :, HALF:]), ACT.Abs)
        hq = keep.tile([P, O], U32, name="hq", align_bytes=64)
        hs = keep.tile([P, O], U8, name="hs", align_bytes=64)
        nc.vector.quantize_mx(hq[:].bitcast(FP8X4), hs[:], hb[:].rearrange("p c t -> p (c t)"))

        for h in range(N // P):
            rows = slice(h * P, (h + 1) * P)
            y_ps = psum.tile([P, O], F32, name="y_ps%d" % h, tag="bank%d" % h)
            nc.tensor.matmul_mx(
                y_ps[:],
                lhsT=wb_w[:, rows].bitcast(FP8X4),
                lhsT_scale=wb_s[:, rows],
                rhs=hq[:].bitcast(FP8X4),
                rhs_scale=hs[:],
                start=True,
                stop=True,
            )
            y = keep.tile([P, O], F32, name="y%d" % h)
            if h == 0:
                nc.vector.tensor_copy(y[:], y_ps[:])
                nc.sync.dma_start(out[rows, :], y[:])
            else:
                nc.scalar.activation(y[:], y_ps[:], ACT.Copy)
                nc.scalar.dma_start(out[rows, :], y[:])
